import numpy as np
import ml_dtypes


def mxq(x, axis, fmt="e4m3"):
    dtype, down = {"e4m3": (ml_dtypes.float8_e4m3fn, 7), "e5m2": (ml_dtypes.float8_e5m2, 14)}[fmt]
    v = np.moveaxis(np.asarray(x, np.float32).astype(ml_dtypes.bfloat16).astype(np.float64), axis, -1)
    blocks = v.reshape(v.shape[:-1] + (-1, 32))
    amax = np.abs(blocks).max(-1, keepdims=True)
    byte = np.maximum(np.where(amax > 0, np.frexp(amax)[1] - 1 + 127, 0) - down, 1)
    scale = np.exp2(byte - 127.0)
    codes = (blocks / scale).astype(np.float32).astype(dtype).astype(np.float64)
    return np.moveaxis((codes * scale).reshape(v.shape), -1, axis)


WIDE = False


def mx_kscale(k):
    if not WIDE:
        return np.ones(k)
    levels = np.array([10, -10, 5, -5, 0])
    if k % 512:
        return np.exp2(np.random.permutation(np.resize(levels, k // 32))).repeat(32)
    a = np.empty((k // 512, 16))
    for p in range(k // 512):
        a[p, :8] = np.random.permutation(np.resize(levels, 8))
        for g in range(8):
            far = levels[np.abs(levels - a[p, g]) >= 10]
            a[p, g + 8] = far[np.random.randint(len(far))]
    return np.exp2(a.ravel()).repeat(32)


def f64(x):
    return np.asarray(x).astype(np.float64)


def striped(idx):
    return np.tile(idx.reshape(-1, 16).T, (8, 1)).astype(np.uint16)


def unstriped(offs):
    return offs[:16].T.reshape(-1).astype(np.int64)


def pack_weight(w):
    k, n = w.shape
    w = f64(np.asarray(w, np.float32).astype(ml_dtypes.bfloat16)).reshape(k // 32, 32, n)
    amax = np.abs(w).max(1)
    byte = np.clip(np.where(amax > 0, np.frexp(amax)[1] - 1 + 127 - 7, 1), 1, 254)
    scaled = (w * np.exp2(127.0 - byte)[:, None, :]).reshape(k, n).astype(np.float32)
    words = np.ascontiguousarray(scaled.reshape(k // 512, 128, 4, n).transpose(0, 1, 3, 2)).astype(ml_dtypes.float8_e4m3fn).view(np.uint8)
    return words, np.ascontiguousarray(byte.astype(np.uint8).reshape(k // 512, 16, n))


def unpack_weight(words, scales):
    g, p, n, _ = words.shape
    vals = np.ascontiguousarray(words).view(ml_dtypes.float8_e4m3fn).astype(np.float64) * np.repeat(np.exp2(scales.astype(np.float64) - 127.0), 8, axis=1)[..., None]
    return vals.transpose(0, 1, 3, 2).reshape(g * 512, n)


E2M1 = np.array([0.0, 0.5, 1.0, 1.5, 2.0, 3.0, 4.0, 6.0, -0.0, -0.5, -1.0, -1.5, -2.0, -3.0, -4.0, -6.0])


def pack_fp4(w):
    k, n = w.shape
    w = f64(np.asarray(w, np.float32).astype(ml_dtypes.bfloat16)).reshape(k // 32, 32, n)
    amax = np.abs(w).max(1)
    mant, ex = np.frexp(amax / 6.0)
    byte = np.clip(np.where(amax > 0, np.where(mant > 0.5, ex, ex - 1) + 127, 1), 1, 254)
    scaled = (w * np.exp2(127.0 - byte)[:, None, :]).reshape(k, n).astype(np.float32)
    c = np.ascontiguousarray(scaled.reshape(k // 512, 128, 4, n).transpose(0, 1, 3, 2)).astype(ml_dtypes.float4_e2m1fn).view(np.uint8) & 0xF
    words = (c[..., 0::2] | (c[..., 1::2] << 4)).reshape(k // 512, 128, 2 * n)
    return np.ascontiguousarray(words), np.ascontiguousarray(byte.astype(np.uint8).reshape(k // 512, 16, n))


def unpack_fp4(words, scales):
    g, _, n = scales.shape
    words = np.ascontiguousarray(words).reshape(g, 128, n, 2)
    nib = np.empty((g, 128, n, 4), np.uint8)
    nib[..., 0::2] = words & 0xF
    nib[..., 1::2] = words >> 4
    vals = E2M1[nib] * np.repeat(np.exp2(scales.astype(np.float64) - 127.0), 8, axis=1)[..., None]
    return vals.transpose(0, 1, 3, 2).reshape(g * 512, n)


def sigmoid(v):
    return 1.0 / (1.0 + np.exp(-np.maximum(v, -700.0)))


K, T, S, N, H = 512, 1024, 512, 256, 512


def setup_inputs():
    n = np.random.standard_normal
    s = mx_kscale(K)[:, None]
    u = mx_kscale(H)
    packed_xT = pack_weight(n((K, T)) * s)
    packed_w1 = pack_fp4(n((K, H)) / np.sqrt(K) / s)
    packed_w2 = pack_fp4(n((K, H)) / np.sqrt(K) / s)
    packed_w3 = pack_fp4(n((H, N)) / np.sqrt(H) / u[:, None])
    return {
        "x_words": packed_xT[0],
        "x_scales": packed_xT[1],
        "w1_words": packed_w1[0],
        "w1_scales": packed_w1[1],
        "w2_words": packed_w2[0],
        "w2_scales": packed_w2[1],
        "lf": (np.random.uniform(0.6, 1.2, (H, S))).astype(np.float32),
        "vf": (np.random.uniform(0.6, 1.2, (H, S))).astype(np.float32),
        "unit": (np.random.uniform(0.6, 1.4, (H, 1)) * u[:, None]).astype(np.float32),
        "w3_words": packed_w3[0],
        "w3_scales": packed_w3[1],
        "offs": striped(np.random.permutation(T)[:S]),
        "abv": striped(np.random.permutation(S)),
        "blw": striped(np.random.permutation(S)),
    }


def reference(x_words, x_scales, w1_words, w1_scales, w2_words, w2_scales, lf, vf, unit, w3_words, w3_scales, offs, abv, blw):
    xq = unpack_weight(x_words, x_scales)[:, unstriped(offs)]
    xl = unpack_fp4(w1_words, w1_scales).T @ xq
    liq = sigmoid(xl)
    xa = liq[:, unstriped(abv)]
    tm = unpack_fp4(w2_words, w2_scales).T @ xq
    vola = 0.6 * (np.log(np.exp(tm) + 1.0)) + 1.2
    vap = (vola * liq) / ((vola - 1.0) * liq + 1.0)
    yb = vap[:, unstriped(blw)]
    dx = f64(lf) * (xa - liq) + f64(vf) * (yb - vap)
    hid = f64(unit) * (dx * vap - (0.4 * vap[:, unstriped(blw)]))
    return unpack_fp4(w3_words, w3_scales).T @ mxq(hid, 0, "e4m3")

@@ -1,0 +1,212 @@
+from contextlib import ExitStack
+
+import concourse.mybir as mybir
+
+K, T, S, N, H = 512, 1024, 512, 256, 512
+FLOPS = 2 * K * H * S * 2 + 2 * H * N * S
+
+F32 = mybir.dt.float32
+BF16 = mybir.dt.bfloat16
+I32 = mybir.dt.int32
+U32 = mybir.dt.uint32
+U16 = mybir.dt.uint16
+U8 = mybir.dt.uint8
+FP8X4 = mybir.dt.float8_e4m3fn_x4
+FP4X4 = mybir.dt.float4_e2m1fn_x4
+ACT = mybir.ActivationFunctionType
+ALU = mybir.AluOpType
+
+P = 128
+PACK = 4
+HALF = S // 2
+CHUNK = 128
+EXP_CAP = 2.0 ** 60
+
+
+def tile_picked_ydisti_mul_p_kernel(
+    tc, x_words, x_scales, w1_words, w1_scales, w2_words, w2_scales, lf, vf, unit,
+    w3_words, w3_scales, offs, abv, blw, out
+):
+    nc = tc.nc
+    with ExitStack() as ctx:
+        lists = ctx.enter_context(tc.tile_pool(name="lists", bufs=1))
+        keep = ctx.enter_context(tc.tile_pool(name="keep", bufs=1))
+        psum = ctx.enter_context(tc.psum_pool(name="psum", bufs=1))
+
+        def load_scales(tile, cols, scales):
+            for q in range(4):
+                nc.sync.dma_start(
+                    tile[32 * q : 32 * q + 4, cols].bitcast(I32),
+                    scales[0, 4 * q : 4 * q + 4, :].bitcast(I32),
+                )
+
+        offs_sb = lists.tile([P, S // 16], U16, name="offs_sb")
+        abv_sb = lists.tile([P, S // 16], U16, name="abv_sb")
+        blw_sb = lists.tile([P, S // 16], U16, name="blw_sb")
+
+        xw = keep.tile([P, T], U32, name="xw", align_bytes=64)
+        xs = keep.tile([P, T], U8, name="xs", align_bytes=64)
+        w_raw = [keep.tile([P, 2 * H], U8, name=f"w_raw{g}", align_bytes=64) for g in range(2)]
+        ws_raw = [keep.tile([P, H], U8, name=f"ws_raw{g}", align_bytes=64) for g in range(2)]
+        w3w = keep.tile([P, 2 * N], U8, name="w3w", align_bytes=64)
+        w3s = keep.tile([P, N], U8, name="w3s", align_bytes=64)
+        nc.vector.memset(xs[:].bitcast(I32), 0)
+        for g in range(2):
+            nc.vector.memset(ws_raw[g][:].bitcast(I32), 0)
+        nc.vector.memset(w3s[:].bitcast(I32), 0)
+
+        nc.sync.dma_start(offs_sb[:], offs)
+        nc.sync.dma_start(xw[:].bitcast(I32), x_words[0].rearrange("p c r -> p (c r)").bitcast(I32))
+        nc.sync.dma_start(w_raw[0][:].bitcast(I32), w1_words[0].bitcast(I32))
+        load_scales(xs, slice(0, T), x_scales)
+        load_scales(ws_raw[0], slice(0, H), w1_scales)
+        nc.sync.dma_start(w_raw[1][:].bitcast(I32), w2_words[0].bitcast(I32))
+        load_scales(ws_raw[1], slice(0, H), w2_scales)
+        nc.sync.dma_start(abv_sb[:], abv)
+        unit_sb = keep.tile([P, PACK], F32, name="unit_sb")
+        nc.sync.dma_start(unit_sb[:], unit.rearrange("(p t) o -> p (t o)", t=PACK))
+        lf_sb = [keep.tile([P, S], F32, name=f"lf{t}") for t in range(PACK)]
+        vf_sb = [keep.tile([P, S], F32, name=f"vf{t}") for t in range(PACK)]
+        for t in range(PACK):
+            nc.sync.dma_start(lf_sb[t][:], lf.rearrange("(p t) j -> p t j", t=PACK)[:, t, :])
+        nc.sync.dma_start(blw_sb[:], blw)
+        for t in range(PACK):
+            nc.sync.dma_start(vf_sb[t][:], vf.rearrange("(p t) j -> p t j", t=PACK)[:, t, :])
+        nc.sync.dma_start(w3w[:].bitcast(I32), w3_words[0].bitcast(I32))
+        load_scales(w3s, slice(0, N), w3_scales)
+
+        w_dealt = [keep.tile([P, 2 * H], U8, name=f"w_dealt{g}", align_bytes=64) for g in range(2)]
+        ws_dealt = [keep.tile([P, H], U8, name=f"ws_dealt{g}", align_bytes=64) for g in range(2)]
+
+        def deal_words(g):
+            nc.vector.tensor_copy(
+                w_dealt[g][:].rearrange("p (t m b) -> p t m b", t=PACK, b=2),
+                w_raw[g][:].rearrange("p (m t b) -> p t m b", t=PACK, b=2),
+            )
+
+        def deal_scales(g):
+            nc.vector.tensor_copy(
+                ws_dealt[g][:].rearrange("p (t m) -> p t m", t=PACK),
+                ws_raw[g][:].rearrange("p (m t) -> p t m", t=PACK),
+            )
+
+        xw_picked = keep.tile([P, S], U32, name="xw_picked", align_bytes=64)
+        xs_picked = keep.tile([P, S], U8, name="xs_picked", align_bytes=64)
+        deal_words(0)
+        nc.vector.tensor_copy(xw_picked[:], xw[:].indirect(offs_sb[:]))
+        nc.vector.tensor_copy(xs_picked[:], xs[:].indirect(offs_sb[:]))
+        deal_scales(0)
+        deal_words(1)
+        deal_scales(1)
+
+        def first_product(g, t, bank):
+            nc.tensor.matmul_mx(
+                out=bank[:],
+                lhsT=w_dealt[g][:, 2 * P * t : 2 * P * (t + 1)].bitcast(FP4X4),
+                lhsT_scale=ws_dealt[g][:, P * t : P * (t + 1)],
+                rhs=xw_picked[:].bitcast(FP8X4),
+                rhs_scale=xs_picked[:],
+                start=True,
+                stop=True,
+            )
+
+        xl = [psum.tile([P, S], F32, name=f"xl{t}") for t in range(PACK)]
+        tm = [psum.tile([P, S], F32, name=f"tm{t}") for t in range(PACK)]
+        for t in range(PACK):
+            first_product(0, t, xl[t])
+        for t in range(PACK):
+            first_product(1, t, tm[t])
+
+        half_unit = keep.tile([P, PACK], F32, name="half_unit")
+        draw_unit = keep.tile([P, PACK], F32, name="draw_unit")
+        nc.gpsimd.tensor_scalar(half_unit[:], unit_sb[:], 0.5, 0.0, ALU.mult, ALU.add)
+        nc.gpsimd.tensor_scalar(draw_unit[:], unit_sb[:], 0.4, 0.0, ALU.mult, ALU.add)
+
+        th = [keep.tile([P, S], F32, name=f"th{t}") for t in range(PACK)]
+        for t in range(PACK):
+            nc.scalar.activation(th[t][:], xl[t][:], ACT.Tanh, scale=0.5)
+        etm = keep.tile([P, PACK, S], F32, name="etm")
+        for t in range(PACK):
+            nc.scalar.activation(etm[:, t, :], tm[t][:], ACT.Exp)
+        capped = keep.tile([P, PACK, S], F32, name="capped")
+        nc.vector.tensor_scalar(
+            capped[:].rearrange("p t j -> p (t j)"), etm[:].rearrange("p t j -> p (t j)"), EXP_CAP, None, ALU.min
+        )
+
+        soft = [keep.tile([P, S], F32, name=f"soft{t}") for t in range(PACK)]
+        for t in range(PACK):
+            nc.scalar.activation(soft[t][:], capped[:, t, :], ACT.Ln, bias=1.0)
+        sp = [keep.tile([P, S], F32, name=f"sp{t}", tag=f"order{t}") for t in range(PACK)]
+        for t in range(PACK):
+            nc.vector.tensor_tensor(sp[t][:], tm[t][:], soft[t][:], ALU.max)
+        lnv = [keep.tile([P, S], F32, name=f"lnv{t}") for t in range(PACK)]
+        for t in range(PACK):
+            nc.scalar.activation(lnv[t][:], sp[t][:], ACT.Ln, scale=0.6, bias=1.2)
+        z = [keep.tile([P, S], F32, name=f"z{t}") for t in range(PACK)]
+        for t in range(PACK):
+            nc.vector.tensor_tensor(z[t][:], xl[t][:], lnv[t][:], ALU.add)
+
+        cl = [keep.tile([P, S], F32, name=f"cl{t}") for t in range(PACK)]
+        for t in range(PACK):
+            th_abv = keep.tile([P, S], F32, name=f"th_abv{t}")
+            for h in range(2):
+                nc.vector.tensor_copy(
+                    th_abv[:, h * HALF : (h + 1) * HALF],
+                    th[t][:].indirect(abv_sb[:, h * (HALF // 16) : (h + 1) * (HALF // 16)]),
+                )
+            da = keep.tile([P, S], F32, name=f"da{t}")
+            nc.vector.tensor_tensor(da[:], th_abv[:], th[t][:], ALU.subtract)
+            nc.vector.scalar_tensor_tensor(cl[t][:], da[:], half_unit[:, t : t + 1], lf_sb[t][:], ALU.mult, ALU.mult)
+
+        vap = [keep.tile([P, S], F32, name=f"vap{t}", tag=f"order{PACK - 1 - t}") for t in range(PACK)]
+        yb = [keep.tile([P, S], F32, name=f"yb{t}") for t in range(PACK)]
+        stay = keep.tile([P, PACK, S], F32, name="stay")
+        move = keep.tile([P, PACK, S], F32, name="move")
+        for t in range(PACK):
+            nc.scalar.activation(vap[t][:], z[t][:], ACT.Sigmoid)
+            for h in range(2):
+                nc.scalar.activation(
+                    yb[t][:, h * HALF : (h + 1) * HALF],
+                    vap[t][:].indirect(blw_sb[:, h * (HALF // 16) : (h + 1) * (HALF // 16)]),
+                    ACT.Copy,
+                )
+            nc.vector.scalar_tensor_tensor(
+                stay[:, t, :], cl[t][:], draw_unit[:, t : t + 1], vap[t][:], ALU.subtract, ALU.mult
+            )
+            wv = keep.tile([P, S], F32, name=f"wv{t}")
+            nc.vector.scalar_tensor_tensor(wv[:], vf_sb[t][:], unit_sb[:, t : t + 1], vap[t][:], ALU.mult, ALU.mult)
+            dv = keep.tile([P, S], F32, name=f"dv{t}")
+            nc.vector.tensor_tensor(dv[:], yb[t][:], vap[t][:], ALU.subtract)
+            nc.vector.scalar_tensor_tensor(
+                move[:, t, :], wv[:], draw_unit[:, t : t + 1], dv[:], ALU.subtract, ALU.mult
+            )
+
+        out_view = out.rearrange("(b p) j -> p b j", p=P)
+        for c in range(S // CHUNK):
+            cols = slice(c * CHUNK, (c + 1) * CHUNK)
+            hid = keep.tile([P, CHUNK, PACK], BF16, name=f"hid{c}", align_bytes=64)
+            nc.vector.tensor_tensor(
+                hid[:].rearrange("p (c i) t -> p c t i", i=4),
+                stay[:, :, cols].rearrange("p t (c i) -> p c t i", i=4),
+                move[:, :, cols].rearrange("p t (c i) -> p c t i", i=4),
+                ALU.add,
+            )
+            codes = keep.tile([P, CHUNK], U32, name=f"codes{c}", align_bytes=64)
+            scales = keep.tile([P, CHUNK], U8, name=f"scales{c}", align_bytes=64)
+            nc.vector.quantize_mx(
+                out=codes[:].bitcast(FP8X4), scales=scales[:], in_=hid[:].rearrange("p j t -> p (j t)")
+            )
+            acc = psum.tile([P, S], F32, name=f"acc{c}", tag=f"tm{c}")
+            for b in range(N // P):
+                nc.tensor.matmul_mx(
+                    out=acc[:, b * CHUNK : (b + 1) * CHUNK],
+                    lhsT=w3w[:, 2 * P * b : 2 * P * (b + 1)].bitcast(FP4X4),
+                    lhsT_scale=w3s[:, P * b : P * (b + 1)],
+                    rhs=codes[:].bitcast(FP8X4),
+                    rhs_scale=scales[:],
+                    start=True,
+                    stop=True,
+                )
+            res = keep.tile([P, N // P, CHUNK], F32, name=f"res{c}")
+            nc.scalar.copy(res[:].rearrange("p b j -> p (b j)"), acc[:, 0 : (N // P) * CHUNK])
+            nc.sync.dma_start(out_view[:, :, cols], res[:])

@@ -31,14 +31,21 @@ def tile_picked_ydisti_mul_p_kernel(
     with ExitStack() as ctx:
         lists = ctx.enter_context(tc.tile_pool(name="lists", bufs=1))
         keep = ctx.enter_context(tc.tile_pool(name="keep", bufs=1))
+        head = ctx.enter_context(tc.tile_pool(name="head", bufs=1))
         psum = ctx.enter_context(tc.psum_pool(name="psum", bufs=1))
 
-        def load_scales(tile, cols, scales):
+        def load_scales(tile, scales):
             for q in range(4):
                 nc.sync.dma_start(
-                    tile[32 * q : 32 * q + 4, cols].bitcast(I32),
+                    tile[32 * q : 32 * q + 4, :].bitcast(I32),
                     scales[0, 4 * q : 4 * q + 4, :].bitcast(I32),
                 )
+
+        def load_scale_rows(queue, tile, scales, q):
+            queue.dma_start(
+                tile[32 * q : 32 * q + 32, :].bitcast(I32),
+                scales[0, 4 * q : 4 * q + 4, :].bitcast(I32).partition_broadcast(8),
+            )
 
         offs_sb = lists.tile([P, S // 16], U16, name="offs_sb")
         abv_sb = lists.tile([P, S // 16], U16, name="abv_sb")
@@ -47,33 +54,38 @@ def tile_picked_ydisti_mul_p_kernel(
         xw = keep.tile([P, T], U32, name="xw", align_bytes=64)
         xs = keep.tile([P, T], U8, name="xs", align_bytes=64)
         w_raw = [keep.tile([P, 2 * H], U8, name=f"w_raw{g}", align_bytes=64) for g in range(2)]
-        ws_raw = [keep.tile([P, H], U8, name=f"ws_raw{g}", align_bytes=64) for g in range(2)]
+        ws_raw = [
+            head.tile([P, H], U8, name="ws_raw0", align_bytes=64, offset=0),
+            keep.tile([P, H], U8, name="ws_raw1", align_bytes=64),
+        ]
         w3w = keep.tile([P, 2 * N], U8, name="w3w", align_bytes=64)
         w3s = keep.tile([P, N], U8, name="w3s", align_bytes=64)
-        nc.vector.memset(xs[:].bitcast(I32), 0)
-        for g in range(2):
-            nc.vector.memset(ws_raw[g][:].bitcast(I32), 0)
-        nc.vector.memset(w3s[:].bitcast(I32), 0)
+        nc.gpsimd.memset(w3s[:].bitcast(I32), 0)
 
         nc.sync.dma_start(offs_sb[:], offs)
-        nc.sync.dma_start(xw[:].bitcast(I32), x_words[0].rearrange("p c r -> p (c r)").bitcast(I32))
+        for q in range(4):
+            load_scale_rows(nc.sync, xs, x_scales, q)
         nc.sync.dma_start(w_raw[0][:].bitcast(I32), w1_words[0].bitcast(I32))
-        load_scales(xs, slice(0, T), x_scales)
-        load_scales(ws_raw[0], slice(0, H), w1_scales)
+        load_scale_rows(nc.sync, ws_raw[0], w1_scales, 0)
+        nc.sync.dma_start(xw[:].bitcast(I32), x_words[0].rearrange("p c r -> p (c r)").bitcast(I32))
+        for q in range(1, 4):
+            load_scale_rows(nc.sync, ws_raw[0], w1_scales, q)
         nc.sync.dma_start(w_raw[1][:].bitcast(I32), w2_words[0].bitcast(I32))
-        load_scales(ws_raw[1], slice(0, H), w2_scales)
+        for q in range(3):
+            load_scale_rows(nc.sync, ws_raw[1], w2_scales, q)
+        load_scale_rows(nc.gpsimd, ws_raw[1], w2_scales, 3)
         nc.sync.dma_start(abv_sb[:], abv)
         unit_sb = keep.tile([P, PACK], F32, name="unit_sb")
-        nc.sync.dma_start(unit_sb[:], unit.rearrange("(p t) o -> p (t o)", t=PACK))
-        lf_sb = [keep.tile([P, S], F32, name=f"lf{t}") for t in range(PACK)]
-        vf_sb = [keep.tile([P, S], F32, name=f"vf{t}") for t in range(PACK)]
-        for t in range(PACK):
-            nc.sync.dma_start(lf_sb[t][:], lf.rearrange("(p t) j -> p t j", t=PACK)[:, t, :])
+        nc.gpsimd.dma_start(unit_sb[:], unit.rearrange("(p t) o -> p (t o)", t=PACK))
+        lf_pair = [keep.tile([P, 2, S], F32, name=f"lf{pair}") for pair in range(2)]
+        vf_pair = [keep.tile([P, 2, S], F32, name=f"vf{pair}") for pair in range(2)]
+        for pair in range(2):
+            nc.sync.dma_start(lf_pair[pair][:], lf.rearrange("(p t) j -> p t j", t=PACK)[:, 2 * pair : 2 * pair + 2, :])
         nc.sync.dma_start(blw_sb[:], blw)
-        for t in range(PACK):
-            nc.sync.dma_start(vf_sb[t][:], vf.rearrange("(p t) j -> p t j", t=PACK)[:, t, :])
+        for pair in range(2):
+            nc.sync.dma_start(vf_pair[pair][:], vf.rearrange("(p t) j -> p t j", t=PACK)[:, 2 * pair : 2 * pair + 2, :])
         nc.sync.dma_start(w3w[:].bitcast(I32), w3_words[0].bitcast(I32))
-        load_scales(w3s, slice(0, N), w3_scales)
+        load_scales(w3s, w3_scales)
 
         w_dealt = [keep.tile([P, 2 * H], U8, name=f"w_dealt{g}", align_bytes=64) for g in range(2)]
         ws_dealt = [keep.tile([P, H], U8, name=f"ws_dealt{g}", align_bytes=64) for g in range(2)]
@@ -90,93 +102,106 @@ def tile_picked_ydisti_mul_p_kernel(
                 ws_raw[g][:].rearrange("p (m t) -> p t m", t=PACK),
             )
 
-        xw_picked = keep.tile([P, S], U32, name="xw_picked", align_bytes=64)
-        xs_picked = keep.tile([P, S], U8, name="xs_picked", align_bytes=64)
+        xw_picked = [keep.tile([P, HALF], U32, name="xw_picked0", align_bytes=64)]
+        xs_picked = [keep.tile([P, HALF], U8, name="xs_picked0", align_bytes=64)]
+
+        def half_list(offsets, h):
+            return offsets[:, h * (HALF // 16) : (h + 1) * (HALF // 16)]
+
+        def pick(picked, table, h):
+            nc.vector.tensor_copy(picked[h][:], table[:].indirect(half_list(offs_sb, h)))
+
         deal_words(0)
-        nc.vector.tensor_copy(xw_picked[:], xw[:].indirect(offs_sb[:]))
-        nc.vector.tensor_copy(xs_picked[:], xs[:].indirect(offs_sb[:]))
+        pick(xs_picked, xs, 0)
+        pick(xw_picked, xw, 0)
         deal_scales(0)
+        xs_picked.append(head.tile([P, HALF], U8, name="xs_picked1", align_bytes=64, offset=0))
+        xw_picked.append(head.tile([P, HALF], U32, name="xw_picked1", align_bytes=64, offset=HALF))
+        pick(xw_picked, xw, 1)
+        pick(xs_picked, xs, 1)
         deal_words(1)
         deal_scales(1)
 
-        def first_product(g, t, bank):
-            nc.tensor.matmul_mx(
-                out=bank[:],
-                lhsT=w_dealt[g][:, 2 * P * t : 2 * P * (t + 1)].bitcast(FP4X4),
-                lhsT_scale=ws_dealt[g][:, P * t : P * (t + 1)],
-                rhs=xw_picked[:].bitcast(FP8X4),
-                rhs_scale=xs_picked[:],
-                start=True,
-                stop=True,
-            )
+        chunks = [(pair, h) for pair in range(2) for h in range(2)]
 
-        xl = [psum.tile([P, S], F32, name=f"xl{t}") for t in range(PACK)]
-        tm = [psum.tile([P, S], F32, name=f"tm{t}") for t in range(PACK)]
-        for t in range(PACK):
-            first_product(0, t, xl[t])
-        for t in range(PACK):
-            first_product(1, t, tm[t])
+        def first_product(g, pair, h, bank):
+            for e in range(2):
+                t = 2 * pair + e
+                nc.tensor.matmul_mx(
+                    out=bank[:, e, :],
+                    lhsT=w_dealt[g][:, 2 * P * t : 2 * P * (t + 1)].bitcast(FP4X4),
+                    lhsT_scale=ws_dealt[g][:, P * t : P * (t + 1)],
+                    rhs=xw_picked[h][:].bitcast(FP8X4),
+                    rhs_scale=xs_picked[h][:],
+                    start=True,
+                    stop=True,
+                )
+
+        def chunk_of(tile, pair, h):
+            return tile[:, 2 * pair : 2 * pair + 2, h * HALF : (h + 1) * HALF]
+
+        xl = {c: psum.tile([P, 2, HALF], F32, name=f"xl{2 * c[0] + c[1]}") for c in chunks}
+        tm = {c: psum.tile([P, 2, HALF], F32, name=f"tm{2 * c[0] + c[1]}") for c in chunks}
+        th = keep.tile([P, PACK, S], F32, name="th")
+        for h in range(2):
+            for pair in range(2):
+                first_product(0, pair, h, xl[pair, h])
+                nc.scalar.activation(chunk_of(th, pair, h), xl[pair, h][:], ACT.Tanh, scale=0.5)
+        capped = {}
+        for c in chunks:
+            first_product(1, c[0], c[1], tm[c])
+            etm = keep.tile([P, 2, HALF], F32, name=f"etm{2 * c[0] + c[1]}")
+            nc.scalar.activation(etm[:], tm[c][:], ACT.Exp)
+            capped[c] = keep.tile([P, 2, HALF], F32, name=f"capped{2 * c[0] + c[1]}")
+            nc.vector.tensor_scalar(capped[c][:], etm[:], EXP_CAP, None, ALU.min)
 
         half_unit = keep.tile([P, PACK], F32, name="half_unit")
         draw_unit = keep.tile([P, PACK], F32, name="draw_unit")
         nc.gpsimd.tensor_scalar(half_unit[:], unit_sb[:], 0.5, 0.0, ALU.mult, ALU.add)
         nc.gpsimd.tensor_scalar(draw_unit[:], unit_sb[:], 0.4, 0.0, ALU.mult, ALU.add)
 
-        th = [keep.tile([P, S], F32, name=f"th{t}") for t in range(PACK)]
-        for t in range(PACK):
-            nc.scalar.activation(th[t][:], xl[t][:], ACT.Tanh, scale=0.5)
-        etm = keep.tile([P, PACK, S], F32, name="etm")
-        for t in range(PACK):
-            nc.scalar.activation(etm[:, t, :], tm[t][:], ACT.Exp)
-        capped = keep.tile([P, PACK, S], F32, name="capped")
-        nc.vector.tensor_scalar(
-            capped[:].rearrange("p t j -> p (t j)"), etm[:].rearrange("p t j -> p (t j)"), EXP_CAP, None, ALU.min
-        )
-
-        soft = [keep.tile([P, S], F32, name=f"soft{t}") for t in range(PACK)]
-        for t in range(PACK):
-            nc.scalar.activation(soft[t][:], capped[:, t, :], ACT.Ln, bias=1.0)
-        sp = [keep.tile([P, S], F32, name=f"sp{t}", tag=f"order{t}") for t in range(PACK)]
-        for t in range(PACK):
-            nc.vector.tensor_tensor(sp[t][:], tm[t][:], soft[t][:], ALU.max)
-        lnv = [keep.tile([P, S], F32, name=f"lnv{t}") for t in range(PACK)]
-        for t in range(PACK):
-            nc.scalar.activation(lnv[t][:], sp[t][:], ACT.Ln, scale=0.6, bias=1.2)
-        z = [keep.tile([P, S], F32, name=f"z{t}") for t in range(PACK)]
-        for t in range(PACK):
-            nc.vector.tensor_tensor(z[t][:], xl[t][:], lnv[t][:], ALU.add)
-
         cl = [keep.tile([P, S], F32, name=f"cl{t}") for t in range(PACK)]
-        for t in range(PACK):
+
+        def liquid_term(t):
             th_abv = keep.tile([P, S], F32, name=f"th_abv{t}")
             for h in range(2):
-                nc.vector.tensor_copy(
-                    th_abv[:, h * HALF : (h + 1) * HALF],
-                    th[t][:].indirect(abv_sb[:, h * (HALF // 16) : (h + 1) * (HALF // 16)]),
-                )
+                nc.vector.tensor_copy(th_abv[:, h * HALF : (h + 1) * HALF], th[:, t, :].indirect(half_list(abv_sb, h)))
             da = keep.tile([P, S], F32, name=f"da{t}")
-            nc.vector.tensor_tensor(da[:], th_abv[:], th[t][:], ALU.subtract)
-            nc.vector.scalar_tensor_tensor(cl[t][:], da[:], half_unit[:, t : t + 1], lf_sb[t][:], ALU.mult, ALU.mult)
+            nc.gpsimd.tensor_tensor(da[:], th_abv[:], th[:, t, :], ALU.subtract)
+            nc.gpsimd.tensor_tensor(cl[t][:], da[:], lf_pair[t // 2][:, t % 2, :], ALU.mult)
 
-        vap = [keep.tile([P, S], F32, name=f"vap{t}", tag=f"order{PACK - 1 - t}") for t in range(PACK)]
-        yb = [keep.tile([P, S], F32, name=f"yb{t}") for t in range(PACK)]
+        sp = keep.tile([P, len(chunks), 2, HALF], F32, name="sp", tag="order")
+        for n, c in enumerate(chunks):
+            soft = keep.tile([P, 2, HALF], F32, name=f"soft{n}")
+            nc.scalar.activation(soft[:], capped[c][:], ACT.Ln, bias=1.0)
+            nc.vector.tensor_tensor(sp[:, n, :, :], tm[c][:], soft[:], ALU.max)
+        for t in range(PACK):
+            liquid_term(t)
+        z = keep.tile([P, PACK, S], F32, name="z")
+        for n, c in enumerate(chunks):
+            lnv = keep.tile([P, 2, HALF], F32, name=f"lnv{n}")
+            nc.scalar.activation(lnv[:], sp[:, n, :, :], ACT.Ln, scale=0.6, bias=1.2)
+            nc.vector.tensor_tensor(chunk_of(z, c[0], c[1]), xl[c][:], lnv[:], ALU.add)
+
+        vap = keep.tile([P, PACK, S], F32, name="vap", tag="order")
         stay = keep.tile([P, PACK, S], F32, name="stay")
         move = keep.tile([P, PACK, S], F32, name="move")
         for t in range(PACK):
-            nc.scalar.activation(vap[t][:], z[t][:], ACT.Sigmoid)
+            yb = keep.tile([P, S], F32, name=f"yb{t}")
+            wv = keep.tile([P, S], F32, name=f"wv{t}")
+            dv = keep.tile([P, S], F32, name=f"dv{t}")
+            vap_unit = keep.tile([P, S], F32, name=f"vap_unit{t}")
+            nc.scalar.activation(vap[:, t, :], z[:, t, :], ACT.Sigmoid)
             for h in range(2):
                 nc.scalar.activation(
-                    yb[t][:, h * HALF : (h + 1) * HALF],
-                    vap[t][:].indirect(blw_sb[:, h * (HALF // 16) : (h + 1) * (HALF // 16)]),
-                    ACT.Copy,
+                    yb[:, h * HALF : (h + 1) * HALF], vap[:, t, :].indirect(half_list(blw_sb, h)), ACT.Copy
                 )
+            nc.scalar.activation(vap_unit[:], vap[:, t, :], ACT.Copy, scale=half_unit[:, t : t + 1])
             nc.vector.scalar_tensor_tensor(
-                stay[:, t, :], cl[t][:], draw_unit[:, t : t + 1], vap[t][:], ALU.subtract, ALU.mult
+                wv[:], vf_pair[t // 2][:, t % 2, :], unit_sb[:, t : t + 1], vap[:, t, :], ALU.mult, ALU.mult
             )
-            wv = keep.tile([P, S], F32, name=f"wv{t}")
-            nc.vector.scalar_tensor_tensor(wv[:], vf_sb[t][:], unit_sb[:, t : t + 1], vap[t][:], ALU.mult, ALU.mult)
-            dv = keep.tile([P, S], F32, name=f"dv{t}")
-            nc.vector.tensor_tensor(dv[:], yb[t][:], vap[t][:], ALU.subtract)
+            nc.vector.tensor_tensor(dv[:], yb[:], vap[:, t, :], ALU.subtract)
+            nc.vector.scalar_tensor_tensor(stay[:, t, :], cl[t][:], 0.8, vap_unit[:], ALU.subtract, ALU.mult)
             nc.vector.scalar_tensor_tensor(
                 move[:, t, :], wv[:], draw_unit[:, t : t + 1], dv[:], ALU.subtract, ALU.mult
             )
@@ -196,10 +221,10 @@ def tile_picked_ydisti_mul_p_kernel(
             nc.vector.quantize_mx(
                 out=codes[:].bitcast(FP8X4), scales=scales[:], in_=hid[:].rearrange("p j t -> p (j t)")
             )
-            acc = psum.tile([P, S], F32, name=f"acc{c}", tag=f"tm{c}")
+            acc = psum.tile([P, 2, HALF], F32, name=f"acc{c}", tag=f"tm{c}")
             for b in range(N // P):
                 nc.tensor.matmul_mx(
-                    out=acc[:, b * CHUNK : (b + 1) * CHUNK],
+                    out=acc[:, 0, b * CHUNK : (b + 1) * CHUNK],
                     lhsT=w3w[:, 2 * P * b : 2 * P * (b + 1)].bitcast(FP4X4),
                     lhsT_scale=w3s[:, P * b : P * (b + 1)],
                     rhs=codes[:].bitcast(FP8X4),
@@ -208,5 +233,5 @@ def tile_picked_ydisti_mul_p_kernel(
                     stop=True,
                 )
             res = keep.tile([P, N // P, CHUNK], F32, name=f"res{c}")
-            nc.scalar.copy(res[:].rearrange("p b j -> p (b j)"), acc[:, 0 : (N // P) * CHUNK])
+            nc.scalar.copy(res[:].rearrange("p b j -> p (b j)"), acc[:, 0, :])
             nc.sync.dma_start(out_view[:, :, cols], res[:])

@@ -20,7 +20,7 @@ P = 128
 PACK = 4
 HALF = S // 2
 CHUNK = 128
-EXP_CAP = 2.0 ** 60
+LOG_FLOOR = 2.0 ** -62
 
 
 def tile_picked_ydisti_mul_p_kernel(
@@ -142,89 +142,114 @@ def tile_picked_ydisti_mul_p_kernel(
 
         xl = {c: psum.tile([P, 2, HALF], F32, name=f"xl{2 * c[0] + c[1]}") for c in chunks}
         tm = {c: psum.tile([P, 2, HALF], F32, name=f"tm{2 * c[0] + c[1]}") for c in chunks}
-        th = keep.tile([P, PACK, S], F32, name="th")
+        liq = keep.tile([P, PACK, S], F32, name="liq")
         for h in range(2):
             for pair in range(2):
                 first_product(0, pair, h, xl[pair, h])
-                nc.scalar.activation(chunk_of(th, pair, h), xl[pair, h][:], ACT.Tanh, scale=0.5)
-        capped = {}
-        for c in chunks:
+                nc.scalar.activation(chunk_of(liq, pair, h), xl[pair, h][:], ACT.Sigmoid)
+        sig_neg = {}
+        for n, c in enumerate(chunks):
             first_product(1, c[0], c[1], tm[c])
-            etm = keep.tile([P, 2, HALF], F32, name=f"etm{2 * c[0] + c[1]}")
-            nc.scalar.activation(etm[:], tm[c][:], ACT.Exp)
-            capped[c] = keep.tile([P, 2, HALF], F32, name=f"capped{2 * c[0] + c[1]}")
-            nc.vector.tensor_scalar(capped[c][:], etm[:], EXP_CAP, None, ALU.min)
-
-        half_unit = keep.tile([P, PACK], F32, name="half_unit")
+            sig_neg[c] = keep.tile([P, 2, HALF], F32, name=f"sig_neg{n}")
+            nc.scalar.activation(sig_neg[c][:], tm[c][:], ACT.Sigmoid, scale=-1.0)
         draw_unit = keep.tile([P, PACK], F32, name="draw_unit")
-        nc.gpsimd.tensor_scalar(half_unit[:], unit_sb[:], 0.5, 0.0, ALU.mult, ALU.add)
         nc.gpsimd.tensor_scalar(draw_unit[:], unit_sb[:], 0.4, 0.0, ALU.mult, ALU.add)
 
-        cl = [keep.tile([P, S], F32, name=f"cl{t}") for t in range(PACK)]
-
-        def liquid_term(t):
-            th_abv = keep.tile([P, S], F32, name=f"th_abv{t}")
-            for h in range(2):
-                nc.vector.tensor_copy(th_abv[:, h * HALF : (h + 1) * HALF], th[:, t, :].indirect(half_list(abv_sb, h)))
-            da = keep.tile([P, S], F32, name=f"da{t}")
-            nc.gpsimd.tensor_tensor(da[:], th_abv[:], th[:, t, :], ALU.subtract)
-            nc.gpsimd.tensor_tensor(cl[t][:], da[:], lf_pair[t // 2][:, t % 2, :], ALU.mult)
-
-        sp = keep.tile([P, len(chunks), 2, HALF], F32, name="sp", tag="order")
+        neg_soft = keep.tile([P, len(chunks), 2, HALF], F32, name="neg_soft", tag="order")
         for n, c in enumerate(chunks):
-            soft = keep.tile([P, 2, HALF], F32, name=f"soft{n}")
-            nc.scalar.activation(soft[:], capped[c][:], ACT.Ln, bias=1.0)
-            nc.vector.tensor_tensor(sp[:, n, :, :], tm[c][:], soft[:], ALU.max)
+            log_sig = keep.tile([P, 2, HALF], F32, name=f"log_sig{n}")
+            nc.scalar.activation(log_sig[:], sig_neg[c][:], ACT.Ln, bias=LOG_FLOOR)
+            nc.vector.scalar_tensor_tensor(neg_soft[:, n, :, :], tm[c][:], -1.0, log_sig[:], ALU.mult, ALU.min)
+
+        cl = [keep.tile([P, S], F32, name=f"cl{t}") for t in range(PACK)]
+        liq_abv = [keep.tile([P, S], F32, name=f"liq_abv{t}") for t in range(PACK)]
         for t in range(PACK):
-            liquid_term(t)
+            for h in range(2):
+                nc.vector.tensor_copy(
+                    liq_abv[t][:, h * HALF : (h + 1) * HALF], liq[:, t, :].indirect(half_list(abv_sb, h))
+                )
+        for t in range(PACK - 1):
+            lf_unit = keep.tile([P, S], F32, name=f"lf_unit{t}")
+            nc.gpsimd.tensor_scalar(
+                lf_unit[:], lf_pair[t // 2][:, t % 2, :], unit_sb[:, t : t + 1], 0.0, ALU.mult, ALU.add
+            )
+            da = keep.tile([P, S], F32, name=f"da{t}")
+            nc.gpsimd.tensor_tensor(da[:], liq_abv[t][:], liq[:, t, :], ALU.subtract)
+            nc.gpsimd.tensor_tensor(cl[t][:], da[:], lf_unit[:], ALU.mult)
+
         z = keep.tile([P, PACK, S], F32, name="z")
         for n, c in enumerate(chunks):
-            lnv = keep.tile([P, 2, HALF], F32, name=f"lnv{n}")
-            nc.scalar.activation(lnv[:], sp[:, n, :, :], ACT.Ln, scale=0.6, bias=1.2)
+            lnv = keep.tile([P, 2, HALF], F32, name=f"lnv{n}", tag=f"lnv{n}")
+            nc.scalar.activation(lnv[:], neg_soft[:, n, :, :], ACT.Ln, scale=-0.6, bias=1.2)
             nc.vector.tensor_tensor(chunk_of(z, c[0], c[1]), xl[c][:], lnv[:], ALU.add)
+
+        last = PACK - 1
+        da_last = keep.tile([P, S], F32, name="da_last", tag=f"lnv{len(chunks) - 2}")
+        nc.vector.tensor_tensor(da_last[:], liq_abv[last][:], liq[:, last, :], ALU.subtract)
+        nc.vector.scalar_tensor_tensor(
+            cl[last][:], da_last[:], unit_sb[:, last : last + 1], lf_pair[1][:, 1, :], ALU.mult, ALU.mult
+        )
 
         vap = keep.tile([P, PACK, S], F32, name="vap", tag="order")
         stay = keep.tile([P, PACK, S], F32, name="stay")
         move = keep.tile([P, PACK, S], F32, name="move")
+        wv = [keep.tile([P, S], F32, name=f"wv{t}") for t in range(PACK)]
+        dv = [keep.tile([P, S], F32, name=f"dv{t}") for t in range(PACK)]
+
+        def move_term(t, cols):
+            nc.vector.scalar_tensor_tensor(
+                move[:, t, cols], wv[t][:, cols], draw_unit[:, t : t + 1], dv[t][:, cols], ALU.subtract, ALU.mult
+            )
+
+        def stay_term(t):
+            nc.vector.scalar_tensor_tensor(
+                stay[:, t, :], cl[t][:], draw_unit[:, t : t + 1], vap[:, t, :], ALU.subtract, ALU.mult
+            )
+
         for t in range(PACK):
             yb = keep.tile([P, S], F32, name=f"yb{t}")
-            wv = keep.tile([P, S], F32, name=f"wv{t}")
-            dv = keep.tile([P, S], F32, name=f"dv{t}")
-            vap_unit = keep.tile([P, S], F32, name=f"vap_unit{t}")
             nc.scalar.activation(vap[:, t, :], z[:, t, :], ACT.Sigmoid)
             for h in range(2):
                 nc.scalar.activation(
                     yb[:, h * HALF : (h + 1) * HALF], vap[:, t, :].indirect(half_list(blw_sb, h)), ACT.Copy
                 )
-            nc.scalar.activation(vap_unit[:], vap[:, t, :], ACT.Copy, scale=half_unit[:, t : t + 1])
             nc.vector.scalar_tensor_tensor(
-                wv[:], vf_pair[t // 2][:, t % 2, :], unit_sb[:, t : t + 1], vap[:, t, :], ALU.mult, ALU.mult
+                wv[t][:], vf_pair[t // 2][:, t % 2, :], unit_sb[:, t : t + 1], vap[:, t, :], ALU.mult, ALU.mult
             )
-            nc.vector.tensor_tensor(dv[:], yb[:], vap[:, t, :], ALU.subtract)
-            nc.vector.scalar_tensor_tensor(stay[:, t, :], cl[t][:], 0.8, vap_unit[:], ALU.subtract, ALU.mult)
-            nc.vector.scalar_tensor_tensor(
-                move[:, t, :], wv[:], draw_unit[:, t : t + 1], dv[:], ALU.subtract, ALU.mult
-            )
+            if t == 0:
+                stay_term(t)
+            else:
+                move_term(t - 1, slice(0, S))
+            nc.vector.tensor_tensor(dv[t][:], yb[:], vap[:, t, :], ALU.subtract)
+            if t > 0:
+                stay_term(t)
+        for h in range(2):
+            move_term(last, slice(h * HALF, (h + 1) * HALF))
 
         out_view = out.rearrange("(b p) j -> p b j", p=P)
-        for c in range(S // CHUNK):
+        hid = [keep.tile([P, CHUNK, PACK], BF16, name=f"hid{c}", align_bytes=64) for c in range(S // CHUNK)]
+
+        def round_hid(c):
             cols = slice(c * CHUNK, (c + 1) * CHUNK)
-            hid = keep.tile([P, CHUNK, PACK], BF16, name=f"hid{c}", align_bytes=64)
             nc.vector.tensor_tensor(
-                hid[:].rearrange("p (c i) t -> p c t i", i=4),
+                hid[c][:].rearrange("p (c i) t -> p c t i", i=4),
                 stay[:, :, cols].rearrange("p t (c i) -> p c t i", i=4),
                 move[:, :, cols].rearrange("p t (c i) -> p c t i", i=4),
                 ALU.add,
             )
+
+        def last_product(c):
+            cols = slice(c * CHUNK, (c + 1) * CHUNK)
             codes = keep.tile([P, CHUNK], U32, name=f"codes{c}", align_bytes=64)
             scales = keep.tile([P, CHUNK], U8, name=f"scales{c}", align_bytes=64)
             nc.vector.quantize_mx(
-                out=codes[:].bitcast(FP8X4), scales=scales[:], in_=hid[:].rearrange("p j t -> p (j t)")
+                out=codes[:].bitcast(FP8X4), scales=scales[:], in_=hid[c][:].rearrange("p j t -> p (j t)")
             )
-            acc = psum.tile([P, 2, HALF], F32, name=f"acc{c}", tag=f"tm{c}")
-            for b in range(N // P):
+            res = keep.tile([P, N // P, CHUNK], F32, name=f"res{c}")
+            for b, bank_tag in enumerate((f"tm{c}", f"xl{c}")):
+                acc = psum.tile([P, CHUNK], F32, name=f"acc{c}_{b}", tag=bank_tag)
                 nc.tensor.matmul_mx(
-                    out=acc[:, 0, b * CHUNK : (b + 1) * CHUNK],
+                    out=acc[:],
                     lhsT=w3w[:, 2 * P * b : 2 * P * (b + 1)].bitcast(FP4X4),
                     lhsT_scale=w3s[:, P * b : P * (b + 1)],
                     rhs=codes[:].bitcast(FP8X4),
@@ -232,6 +257,11 @@ def tile_picked_ydisti_mul_p_kernel(
                     start=True,
                     stop=True,
                 )
-            res = keep.tile([P, N // P, CHUNK], F32, name=f"res{c}")
-            nc.scalar.copy(res[:].rearrange("p b j -> p (b j)"), acc[:, 0, :])
+                nc.scalar.copy(res[:, b, :], acc[:])
             nc.sync.dma_start(out_view[:, :, cols], res[:])
+
+        round_hid(0)
+        for c in range(S // CHUNK):
+            if c + 1 < S // CHUNK:
+                round_hid(c + 1)
+            last_product(c)

from contextlib import ExitStack

import concourse.mybir as mybir

K, T, S, N, H = 512, 1024, 512, 256, 512
FLOPS = 2 * K * H * S * 2 + 2 * H * N * S

F32 = mybir.dt.float32
BF16 = mybir.dt.bfloat16
I32 = mybir.dt.int32
U32 = mybir.dt.uint32
U16 = mybir.dt.uint16
U8 = mybir.dt.uint8
FP8X4 = mybir.dt.float8_e4m3fn_x4
FP4X4 = mybir.dt.float4_e2m1fn_x4
ACT = mybir.ActivationFunctionType
ALU = mybir.AluOpType

P = 128
PACK = 4
HALF = S // 2
CHUNK = 128
LOG_FLOOR = 2.0 ** -62


def tile_picked_ydisti_mul_p_kernel(
    tc, x_words, x_scales, w1_words, w1_scales, w2_words, w2_scales, lf, vf, unit,
    w3_words, w3_scales, offs, abv, blw, out
):
    nc = tc.nc
    with ExitStack() as ctx:
        lists = ctx.enter_context(tc.tile_pool(name="lists", bufs=1))
        keep = ctx.enter_context(tc.tile_pool(name="keep", bufs=1))
        head = ctx.enter_context(tc.tile_pool(name="head", bufs=1))
        psum = ctx.enter_context(tc.psum_pool(name="psum", bufs=1))

        def load_scales(tile, scales):
            for q in range(4):
                nc.sync.dma_start(
                    tile[32 * q : 32 * q + 4, :].bitcast(I32),
                    scales[0, 4 * q : 4 * q + 4, :].bitcast(I32),
                )

        def load_scale_rows(queue, tile, scales, q):
            queue.dma_start(
                tile[32 * q : 32 * q + 32, :].bitcast(I32),
                scales[0, 4 * q : 4 * q + 4, :].bitcast(I32).partition_broadcast(8),
            )

        offs_sb = lists.tile([P, S // 16], U16, name="offs_sb")
        abv_sb = lists.tile([P, S // 16], U16, name="abv_sb")
        blw_sb = lists.tile([P, S // 16], U16, name="blw_sb")

        xw = keep.tile([P, T], U32, name="xw", align_bytes=64)
        xs = keep.tile([P, T], U8, name="xs", align_bytes=64)
        w_raw = [keep.tile([P, 2 * H], U8, name=f"w_raw{g}", align_bytes=64) for g in range(2)]
        ws_raw = [
            head.tile([P, H], U8, name="ws_raw0", align_bytes=64, offset=0),
            keep.tile([P, H], U8, name="ws_raw1", align_bytes=64),
        ]
        w3w = keep.tile([P, 2 * N], U8, name="w3w", align_bytes=64)
        w3s = keep.tile([P, N], U8, name="w3s", align_bytes=64)
        nc.gpsimd.memset(w3s[:].bitcast(I32), 0)

        nc.sync.dma_start(offs_sb[:], offs)
        for q in range(4):
            load_scale_rows(nc.sync, xs, x_scales, q)
        nc.sync.dma_start(w_raw[0][:].bitcast(I32), w1_words[0].bitcast(I32))
        load_scale_rows(nc.sync, ws_raw[0], w1_scales, 0)
        nc.sync.dma_start(xw[:].bitcast(I32), x_words[0].rearrange("p c r -> p (c r)").bitcast(I32))
        for q in range(1, 4):
            load_scale_rows(nc.sync, ws_raw[0], w1_scales, q)
        nc.sync.dma_start(w_raw[1][:].bitcast(I32), w2_words[0].bitcast(I32))
        for q in range(3):
            load_scale_rows(nc.sync, ws_raw[1], w2_scales, q)
        load_scale_rows(nc.gpsimd, ws_raw[1], w2_scales, 3)
        nc.sync.dma_start(abv_sb[:], abv)
        unit_sb = keep.tile([P, PACK], F32, name="unit_sb")
        nc.gpsimd.dma_start(unit_sb[:], unit.rearrange("(p t) o -> p (t o)", t=PACK))
        lf_pair = [keep.tile([P, 2, S], F32, name=f"lf{pair}") for pair in range(2)]
        vf_pair = [keep.tile([P, 2, S], F32, name=f"vf{pair}") for pair in range(2)]
        for pair in range(2):
            nc.sync.dma_start(lf_pair[pair][:], lf.rearrange("(p t) j -> p t j", t=PACK)[:, 2 * pair : 2 * pair + 2, :])
        nc.sync.dma_start(blw_sb[:], blw)
        for pair in range(2):
            nc.sync.dma_start(vf_pair[pair][:], vf.rearrange("(p t) j -> p t j", t=PACK)[:, 2 * pair : 2 * pair + 2, :])
        nc.sync.dma_start(w3w[:].bitcast(I32), w3_words[0].bitcast(I32))
        load_scales(w3s, w3_scales)

        w_dealt = [keep.tile([P, 2 * H], U8, name=f"w_dealt{g}", align_bytes=64) for g in range(2)]
        ws_dealt = [keep.tile([P, H], U8, name=f"ws_dealt{g}", align_bytes=64) for g in range(2)]

        def deal_words(g):
            nc.vector.tensor_copy(
                w_dealt[g][:].rearrange("p (t m b) -> p t m b", t=PACK, b=2),
                w_raw[g][:].rearrange("p (m t b) -> p t m b", t=PACK, b=2),
            )

        def deal_scales(g):
            nc.vector.tensor_copy(
                ws_dealt[g][:].rearrange("p (t m) -> p t m", t=PACK),
                ws_raw[g][:].rearrange("p (m t) -> p t m", t=PACK),
            )

        xw_picked = [keep.tile([P, HALF], U32, name="xw_picked0", align_bytes=64)]
        xs_picked = [keep.tile([P, HALF], U8, name="xs_picked0", align_bytes=64)]

        def half_list(offsets, h):
            return offsets[:, h * (HALF // 16) : (h + 1) * (HALF // 16)]

        def pick(picked, table, h):
            nc.vector.tensor_copy(picked[h][:], table[:].indirect(half_list(offs_sb, h)))

        deal_words(0)
        pick(xs_picked, xs, 0)
        pick(xw_picked, xw, 0)
        deal_scales(0)
        xs_picked.append(head.tile([P, HALF], U8, name="xs_picked1", align_bytes=64, offset=0))
        xw_picked.append(head.tile([P, HALF], U32, name="xw_picked1", align_bytes=64, offset=HALF))
        pick(xw_picked, xw, 1)
        pick(xs_picked, xs, 1)
        deal_words(1)
        deal_scales(1)

        chunks = [(pair, h) for pair in range(2) for h in range(2)]

        def first_product(g, pair, h, bank):
            for e in range(2):
                t = 2 * pair + e
                nc.tensor.matmul_mx(
                    out=bank[:, e, :],
                    lhsT=w_dealt[g][:, 2 * P * t : 2 * P * (t + 1)].bitcast(FP4X4),
                    lhsT_scale=ws_dealt[g][:, P * t : P * (t + 1)],
                    rhs=xw_picked[h][:].bitcast(FP8X4),
                    rhs_scale=xs_picked[h][:],
                    start=True,
                    stop=True,
                )

        def chunk_of(tile, pair, h):
            return tile[:, 2 * pair : 2 * pair + 2, h * HALF : (h + 1) * HALF]

        xl = {c: psum.tile([P, 2, HALF], F32, name=f"xl{2 * c[0] + c[1]}") for c in chunks}
        tm = {c: psum.tile([P, 2, HALF], F32, name=f"tm{2 * c[0] + c[1]}") for c in chunks}
        liq = keep.tile([P, PACK, S], F32, name="liq")
        for h in range(2):
            for pair in range(2):
                first_product(0, pair, h, xl[pair, h])
                nc.scalar.activation(chunk_of(liq, pair, h), xl[pair, h][:], ACT.Sigmoid)
        sig_neg = {}
        for n, c in enumerate(chunks):
            first_product(1, c[0], c[1], tm[c])
            sig_neg[c] = keep.tile([P, 2, HALF], F32, name=f"sig_neg{n}")
            nc.scalar.activation(sig_neg[c][:], tm[c][:], ACT.Sigmoid, scale=-1.0)
        draw_unit = keep.tile([P, PACK], F32, name="draw_unit")
        nc.gpsimd.tensor_scalar(draw_unit[:], unit_sb[:], 0.4, 0.0, ALU.mult, ALU.add)

        neg_soft = keep.tile([P, len(chunks), 2, HALF], F32, name="neg_soft", tag="order")
        for n, c in enumerate(chunks):
            log_sig = keep.tile([P, 2, HALF], F32, name=f"log_sig{n}")
            nc.scalar.activation(log_sig[:], sig_neg[c][:], ACT.Ln, bias=LOG_FLOOR)
            nc.vector.scalar_tensor_tensor(neg_soft[:, n, :, :], tm[c][:], -1.0, log_sig[:], ALU.mult, ALU.min)

        cl = [keep.tile([P, S], F32, name=f"cl{t}") for t in range(PACK)]
        liq_abv = [keep.tile([P, S], F32, name=f"liq_abv{t}") for t in range(PACK)]
        for t in range(PACK):
            for h in range(2):
                nc.vector.tensor_copy(
                    liq_abv[t][:, h * HALF : (h + 1) * HALF], liq[:, t, :].indirect(half_list(abv_sb, h))
                )
        for t in range(PACK - 1):
            lf_unit = keep.tile([P, S], F32, name=f"lf_unit{t}")
            nc.gpsimd.tensor_scalar(
                lf_unit[:], lf_pair[t // 2][:, t % 2, :], unit_sb[:, t : t + 1], 0.0, ALU.mult, ALU.add
            )
            da = keep.tile([P, S], F32, name=f"da{t}")
            nc.gpsimd.tensor_tensor(da[:], liq_abv[t][:], liq[:, t, :], ALU.subtract)
            nc.gpsimd.tensor_tensor(cl[t][:], da[:], lf_unit[:], ALU.mult)

        z = keep.tile([P, PACK, S], F32, name="z")
        for n, c in enumerate(chunks):
            lnv = keep.tile([P, 2, HALF], F32, name=f"lnv{n}", tag=f"lnv{n}")
            nc.scalar.activation(lnv[:], neg_soft[:, n, :, :], ACT.Ln, scale=-0.6, bias=1.2)
            nc.vector.tensor_tensor(chunk_of(z, c[0], c[1]), xl[c][:], lnv[:], ALU.add)

        last = PACK - 1
        da_last = keep.tile([P, S], F32, name="da_last", tag=f"lnv{len(chunks) - 2}")
        nc.vector.tensor_tensor(da_last[:], liq_abv[last][:], liq[:, last, :], ALU.subtract)
        nc.vector.scalar_tensor_tensor(
            cl[last][:], da_last[:], unit_sb[:, last : last + 1], lf_pair[1][:, 1, :], ALU.mult, ALU.mult
        )

        vap = keep.tile([P, PACK, S], F32, name="vap", tag="order")
        stay = keep.tile([P, PACK, S], F32, name="stay")
        move = keep.tile([P, PACK, S], F32, name="move")
        wv = [keep.tile([P, S], F32, name=f"wv{t}") for t in range(PACK)]
        dv = [keep.tile([P, S], F32, name=f"dv{t}") for t in range(PACK)]

        def move_term(t, cols):
            nc.vector.scalar_tensor_tensor(
                move[:, t, cols], wv[t][:, cols], draw_unit[:, t : t + 1], dv[t][:, cols], ALU.subtract, ALU.mult
            )

        def stay_term(t):
            nc.vector.scalar_tensor_tensor(
                stay[:, t, :], cl[t][:], draw_unit[:, t : t + 1], vap[:, t, :], ALU.subtract, ALU.mult
            )

        for t in range(PACK):
            yb = keep.tile([P, S], F32, name=f"yb{t}")
            nc.scalar.activation(vap[:, t, :], z[:, t, :], ACT.Sigmoid)
            for h in range(2):
                nc.scalar.activation(
                    yb[:, h * HALF : (h + 1) * HALF], vap[:, t, :].indirect(half_list(blw_sb, h)), ACT.Copy
                )
            nc.vector.scalar_tensor_tensor(
                wv[t][:], vf_pair[t // 2][:, t % 2, :], unit_sb[:, t : t + 1], vap[:, t, :], ALU.mult, ALU.mult
            )
            if t == 0:
                stay_term(t)
            else:
                move_term(t - 1, slice(0, S))
            nc.vector.tensor_tensor(dv[t][:], yb[:], vap[:, t, :], ALU.subtract)
            if t > 0:
                stay_term(t)
        for h in range(2):
            move_term(last, slice(h * HALF, (h + 1) * HALF))

        out_view = out.rearrange("(b p) j -> p b j", p=P)
        hid = [keep.tile([P, CHUNK, PACK], BF16, name=f"hid{c}", align_bytes=64) for c in range(S // CHUNK)]

        def round_hid(c):
            cols = slice(c * CHUNK, (c + 1) * CHUNK)
            nc.vector.tensor_tensor(
                hid[c][:].rearrange("p (c i) t -> p c t i", i=4),
                stay[:, :, cols].rearrange("p t (c i) -> p c t i", i=4),
                move[:, :, cols].rearrange("p t (c i) -> p c t i", i=4),
                ALU.add,
            )

        def last_product(c):
            cols = slice(c * CHUNK, (c + 1) * CHUNK)
            codes = keep.tile([P, CHUNK], U32, name=f"codes{c}", align_bytes=64)
            scales = keep.tile([P, CHUNK], U8, name=f"scales{c}", align_bytes=64)
            nc.vector.quantize_mx(
                out=codes[:].bitcast(FP8X4), scales=scales[:], in_=hid[c][:].rearrange("p j t -> p (j t)")
            )
            res = keep.tile([P, N // P, CHUNK], F32, name=f"res{c}")
            for b, bank_tag in enumerate((f"tm{c}", f"xl{c}")):
                acc = psum.tile([P, CHUNK], F32, name=f"acc{c}_{b}", tag=bank_tag)
                nc.tensor.matmul_mx(
                    out=acc[:],
                    lhsT=w3w[:, 2 * P * b : 2 * P * (b + 1)].bitcast(FP4X4),
                    lhsT_scale=w3s[:, P * b : P * (b + 1)],
                    rhs=codes[:].bitcast(FP8X4),
                    rhs_scale=scales[:],
                    start=True,
                    stop=True,
                )
                nc.scalar.copy(res[:, b, :], acc[:])
            nc.sync.dma_start(out_view[:, :, cols], res[:])

        round_hid(0)
        for c in range(S // CHUNK):
            if c + 1 < S // CHUNK:
                round_hid(c + 1)
            last_product(c)
